import numpy as np
import ml_dtypes


def mxq(x, axis, fmt="e4m3"):
    dtype, down = {"e4m3": (ml_dtypes.float8_e4m3fn, 7), "e5m2": (ml_dtypes.float8_e5m2, 14)}[fmt]
    v = np.moveaxis(np.asarray(x, np.float32).astype(ml_dtypes.bfloat16).astype(np.float64), axis, -1)
    blocks = v.reshape(v.shape[:-1] + (-1, 32))
    amax = np.abs(blocks).max(-1, keepdims=True)
    byte = np.maximum(np.where(amax > 0, np.frexp(amax)[1] - 1 + 127, 0) - down, 1)
    scale = np.exp2(byte - 127.0)
    codes = (blocks / scale).astype(np.float32).astype(dtype).astype(np.float64)
    return np.moveaxis((codes * scale).reshape(v.shape), -1, axis)


WIDE = False


def mx_kscale(k):
    if not WIDE:
        return np.ones(k)
    levels = np.array([30, -30])
    if k % 512:
        return np.exp2(np.random.permutation(np.resize(levels, k // 32))).repeat(32)
    a = np.empty((k // 512, 16))
    for p in range(k // 512):
        a[p, :8] = np.random.permutation(np.resize(levels, 8))
        for g in range(8):
            far = levels[np.abs(levels - a[p, g]) >= 10]
            a[p, g + 8] = far[np.random.randint(len(far))]
    return np.exp2(a.ravel()).repeat(32)


BF16 = ml_dtypes.bfloat16


def bf(x):
    return np.asarray(x, np.float32).astype(BF16)


def f64(x):
    return np.asarray(x).astype(np.float64)


M, N, D, H = 1024, 2048, 1024, 512
CAP = 2.0
TAIL = 4.0


def setup_inputs():
    s = mx_kscale(D)
    t = mx_kscale(H)
    std_u = np.sqrt(TAIL / (TAIL - 2.0))
    q = np.random.standard_normal((M, D))
    k = np.random.standard_normal((N, D)) / np.sqrt(D)
    u = np.random.standard_t(TAIL, (H, M)) / std_u
    p = np.random.standard_normal((H, N)) / np.sqrt(H)
    return {"q": bf(q * s),
            "k": bf(k / s),
            "u": bf(u * t[:, None]),
            "p": bf(p / t[:, None]),
            "b": bf(0.3 * np.random.standard_normal(N))}


def reference(q, k, u, p, b):
    content = mxq(f64(q), 1, "e4m3") @ mxq(f64(k), 1, "e4m3").T
    intensity = mxq(f64(u), 0, "e5m2").T @ mxq(f64(p), 0, "e4m3")
    logits = content + intensity + f64(b)
    e = np.exp(CAP * np.tanh(logits / CAP))
    z = np.mean(e, axis=1, keepdims=True)
    return e, z

@@ -1,0 +1,286 @@
+from contextlib import ExitStack
+
+import concourse.mybir as mybir
+from concourse.masks import make_identity
+
+M, N, D, H = 1024, 2048, 1024, 512
+FLOPS = 2 * M * N * (D + H)
+CAP = 2.0
+
+F32 = mybir.dt.float32
+BF16 = mybir.dt.bfloat16
+U32 = mybir.dt.uint32
+U8 = mybir.dt.uint8
+E4M3X4 = mybir.dt.float8_e4m3fn_x4
+E5M2X4 = mybir.dt.float8_e5m2_x4
+ACT = mybir.ActivationFunctionType
+ALU = mybir.AluOpType
+
+P = 128
+PACK = 4
+K_PASS = P * PACK
+G = D // K_PASS
+NT = 512
+MB = M // P
+NB = N // NT
+RB = NT // P
+STEPS = MB * NB
+SCALAR_JOBS = 15
+PW = NT // 2
+WARM_UPS = 5
+SCALAR_U = 0
+PROMPT = 2
+RUN_STEPS = [0, 1, 3, 4, 5, 9, 13, 17, 21]
+U_STEP = -2
+P_STEPS = [4, 6, 10, 14, 18, 22]
+
+
+def tile_softcapped_attention_weights_s2_kernel(tc, q, k, u, p, b, out_0, out_1):
+    nc = tc.nc
+    with ExitStack() as ctx:
+        keep = ctx.enter_context(tc.tile_pool(name="keep", bufs=1))
+        stage = ctx.enter_context(tc.tile_pool(name="stage", bufs=5))
+        work = ctx.enter_context(tc.tile_pool(name="work", bufs=16))
+        psum = ctx.enter_context(tc.psum_pool(name="psum", bufs=4))
+        ctx.enter_context(tc.manual_schedule(engines={mybir.EngineType.PE, mybir.EngineType.SP}))
+
+        def mx_tiles(name, width):
+            codes = keep.tile([P, width], U32, name=name + "_codes", align_bytes=64)
+            scales = keep.tile([P, width], U8, name=name + "_scales", align_bytes=64)
+            return codes, scales
+
+        q_mx = [mx_tiles("q%d" % m, G * P) for m in range(MB)]
+        k_mx = [[mx_tiles("k%d_%d" % (n, g), NT) for g in range(G)] for n in range(NB)]
+        u_mx = [mx_tiles("u%d" % m, P) for m in range(MB)]
+        p_mx = [mx_tiles("p%d" % n, NT) for n in range(NB)]
+
+        ident = keep.tile([P, P], F32, name="ident")
+        make_identity(nc, ident[:])
+        ones = keep.tile([P, P], BF16, name="ones")
+        nc.vector.memset(ones[:], 1.0)
+        b_row = keep.tile([P, N], BF16, name="b_row")
+        zeros = keep.tile([P, NT], BF16, name="zeros")
+        nc.vector.memset(zeros[:], 0.0)
+        nc.vector.memset(b_row[:], 0.0)
+        idle = psum.tile([P, NT], F32, name="idle", tag="acc")
+        for i in range(WARM_UPS):
+            nc.tensor.matmul(idle[:], lhsT=ones[:], rhs=zeros[:], start=True, stop=True)
+        warm = keep.tile([P, 1], F32, name="warm")
+        nc.scalar.activation(out=warm[:], in_=ones[:, 0:1], func=ACT.Tanh)
+        sums = []
+        for n in range(NB):
+            sums_n = keep.tile([P, P], F32, name="sums%d" % n)
+            nc.gpsimd.memset(sums_n[:], 0.0)
+            sums.append(sums_n)
+
+        jobs = [("k", 0, r) for r in range(RB)] + [("q", m, 0) for m in range(MB)]
+        jobs = jobs + [("k", n, r) for n in range(1, NB) for r in range(RB)]
+        raw, p_raw, u_raw = {}, {}, {}
+
+        def load_rows(job):
+            kind, i, r = job
+            rows = keep.tile([P, D], BF16, name="raw_%s%d_%d" % job)
+            src = q[i * P:(i + 1) * P, :] if kind == "q" else k[i * NT + r * P:i * NT + (r + 1) * P, :]
+            nc.sync.dma_start(out=rows[:], in_=src)
+            raw[job] = rows
+
+        def load_p(n, h0, h1):
+            rows = keep.tile([P, PACK, (h1 - h0) * PW], BF16, name="p_raw%d_%d" % (n, h0))
+            src = p[:, n * NT + h0 * PW:n * NT + h1 * PW]
+            nc.sync.dma_start(out=rows[:], in_=src.rearrange("(p t) c -> p t c", t=PACK))
+            for h in range(h0, h1):
+                p_raw[(n, h)] = rows[:, :, (h - h0) * PW:(h - h0 + 1) * PW]
+
+        def load_u(m0, m1):
+            rows = keep.tile([P, PACK, (m1 - m0) * P], BF16, name="u_raw%d" % m0)
+            nc.sync.dma_start(out=rows[:], in_=u[:, m0 * P:m1 * P].rearrange("(p t) c -> p t c", t=PACK))
+            for m in range(m0, m1):
+                u_raw[m] = rows[:, :, (m - m0) * P:(m - m0 + 1) * P]
+
+        load_rows(jobs[0])
+        nc.sync.dma_start(out=b_row[0:1, :], in_=b.rearrange("(o n) -> o n", o=1))
+        load_p(0, 0, 1)
+        for job in jobs[1:RB + 1]:
+            load_rows(job)
+        load_p(0, 1, 2)
+        load_u(0, 1)
+        for job in jobs[RB + 1:RB + 3]:
+            load_rows(job)
+        load_u(1, MB // 2)
+        for job in jobs[RB + 3:RB + MB // 2 + 2]:
+            load_rows(job)
+        load_u(MB // 2, MB)
+        for job in jobs[RB + MB // 2 + 2:RB + MB]:
+            load_rows(job)
+        for n in range(1, NB):
+            load_p(n, 0, 2)
+            for r in range(RB):
+                load_rows(("k", n, r))
+
+        banks, turned, woven, acc, tiles = {}, {}, {}, {}, {}
+        bias = {}
+
+        def transpose(job):
+            words = raw[job][:].bitcast(F32)
+            bank = psum.tile([P, G, 2, P], F32, name="bank", tag="turn")
+            for g in range(G):
+                for h in range(2):
+                    nc.tensor.transpose(bank[:, g, h, :], words[:, 256 * g + h:256 * (g + 1):2], ident[:])
+            banks[job] = bank
+
+        def copy_out(job):
+            dst = stage.tile([P, G * P * PACK], BF16, name="turned", align_bytes=64)
+            view = dst[:].bitcast(F32).rearrange("p (g r h) -> p g r h", g=G, h=2)
+            src = banks[job][:].rearrange("p g h r -> p g r h")
+            if jobs.index(job) < SCALAR_JOBS:
+                nc.scalar.copy(out=view, in_=src)
+            else:
+                nc.vector.tensor_copy(out=view, in_=src)
+            turned[job] = dst
+
+        def quantize_rows(job):
+            kind, i, r = job
+            if kind == "q":
+                codes, scales = q_mx[i]
+                nc.vector.quantize_mx(out=codes[:].bitcast(E4M3X4), scales=scales[:], in_=turned[job][:])
+            else:
+                for g in range(G):
+                    codes, scales = k_mx[i][g]
+                    cols = slice(r * P, (r + 1) * P)
+                    nc.vector.quantize_mx(out=codes[:, cols].bitcast(E4M3X4), scales=scales[:, cols],
+                                          in_=turned[job][:, g * K_PASS:(g + 1) * K_PASS])
+
+        def weave(key, src, copy):
+            width = src.shape[2]
+            dst = stage.tile([P, width * PACK], BF16, name="woven_%s%d" % (key[0], width), align_bytes=64)
+            copy(out=dst[:].rearrange("p (c i t) -> p c t i", i=4, t=PACK), in_=src.rearrange("p t (c i) -> p c t i", i=4))
+            woven[key] = dst
+
+        def weave_u(m):
+            weave(("u", m), u_raw[m], nc.scalar.copy if m < SCALAR_U else nc.vector.tensor_copy)
+
+        def weave_p(n, h):
+            weave(("p", n, h), p_raw[(n, h)], nc.vector.tensor_copy)
+
+        def quantize_u(m):
+            codes, scales = u_mx[m]
+            nc.vector.quantize_mx(out=codes[:].bitcast(E5M2X4), scales=scales[:], in_=woven[("u", m)][:])
+
+        def quantize_p(n, h):
+            codes, scales = p_mx[n]
+            cols = slice(h * PW, (h + 1) * PW)
+            nc.vector.quantize_mx(out=codes[:, cols].bitcast(E4M3X4), scales=scales[:, cols], in_=woven[("p", n, h)][:])
+
+        def spread_bias(n):
+            bank = psum.tile([P, NT], BF16, name="bias_bank", tag="acc")
+            nc.tensor.matmul(bank[:], lhsT=ones[:], rhs=b_row[:, n * NT:(n + 1) * NT], start=True, stop=True)
+            banks[n] = bank
+
+        def keep_bias(n):
+            bias_n = keep.tile([P, NT], BF16, name="bias%d" % n)
+            nc.scalar.copy(out=bias_n[:], in_=banks[n][:])
+            bias[n] = bias_n
+
+        def multiply(s):
+            n, m = divmod(s, MB)
+            bank = psum.tile([P, NT], F32, name="acc", tag="acc")
+            for g in range(G):
+                cols = slice(g * P, (g + 1) * P)
+                nc.tensor.matmul_mx(out=bank[:], lhsT=q_mx[m][0][:, cols].bitcast(E4M3X4), lhsT_scale=q_mx[m][1][:, cols],
+                                    rhs=k_mx[n][g][0][:].bitcast(E4M3X4), rhs_scale=k_mx[n][g][1][:],
+                                    start=(g == 0), stop=False)
+            nc.tensor.matmul_mx(out=bank[:], lhsT=u_mx[m][0][:].bitcast(E5M2X4), lhsT_scale=u_mx[m][1][:],
+                                rhs=p_mx[n][0][:].bitcast(E4M3X4), rhs_scale=p_mx[n][1][:], start=False, stop=True)
+            acc[s] = bank
+
+        def add_bias(s):
+            logits = work.tile([P, NT], F32, name="logits")
+            nc.vector.tensor_tensor(out=logits[:], in0=acc[s][:], in1=bias[s // MB][:], op=ALU.add)
+            tiles[s] = logits
+
+        def cap(s):
+            nc.scalar.activation(out=tiles[s][:], in_=tiles[s][:], func=ACT.Tanh, scale=1.0 / CAP)
+
+        def weigh(s):
+            n, m = divmod(s, MB)
+            nc.scalar.activation(out=tiles[s][:], in_=tiles[s][:], func=ACT.Exp, scale=CAP,
+                                 accum_out=sums[n][:, m:m + 1])
+            nc.sync.dma_start(out=out_0[m * P:(m + 1) * P, n * NT:(n + 1) * NT], in_=tiles[s][:])
+
+        k0 = jobs[:RB]
+        q0, q1, q2 = jobs[RB:RB + 3]
+        transpose(k0[0])
+        for n in range(NB):
+            spread_bias(n)
+        copy_out(k0[0])
+        for n in range(NB):
+            keep_bias(n)
+        weave_p(0, 0)
+        quantize_rows(k0[0])
+        quantize_p(0, 0)
+        for job in k0[1:3]:
+            transpose(job)
+            copy_out(job)
+            quantize_rows(job)
+        for job in (k0[3], q0):
+            transpose(job)
+            copy_out(job)
+        weave_p(0, 1)
+        weave_u(0)
+        quantize_rows(k0[3])
+        quantize_rows(q0)
+        quantize_p(0, 1)
+        quantize_u(0)
+        for job in (q1, q2):
+            transpose(job)
+            copy_out(job)
+        weave_u(1)
+        quantize_rows(q1)
+        quantize_u(1)
+        quantize_rows(q2)
+
+        rest = jobs[RB + 3:]
+        turn_at = {job: RUN_STEPS[j // 2] for j, job in enumerate(rest)}
+        copy_at = {job: turn_at[job] + (0 if turn_at[job] < PROMPT else 1) for job in rest}
+        u_at = {m: m + U_STEP for m in range(2, MB)}
+        p_at = {(n, h): P_STEPS[2 * (n - 1) + h] for n in range(1, NB) for h in range(2)}
+        z_bank = None
+        for t in range(STEPS + 3):
+            s = t
+            if 0 <= s < STEPS:
+                multiply(s)
+            for job in rest:
+                if turn_at[job] == t:
+                    transpose(job)
+            if 0 <= s - 1 < STEPS:
+                add_bias(s - 1)
+            if 0 <= s - 2 < STEPS:
+                cap(s - 2)
+            if 0 <= s - 3 < STEPS:
+                weigh(s - 3)
+            for piece in p_at:
+                if p_at[piece] == t - 1:
+                    quantize_p(*piece)
+            for m in u_at:
+                if u_at[m] == t - 1:
+                    quantize_u(m)
+            for job in rest:
+                if copy_at[job] == t - 1:
+                    quantize_rows(job)
+            for job in rest:
+                if copy_at[job] == t:
+                    copy_out(job)
+            for piece in p_at:
+                if p_at[piece] == t:
+                    weave_p(*piece)
+            for m in u_at:
+                if u_at[m] == t:
+                    weave_u(m)
+            if s == STEPS:
+                z_bank = psum.tile([P, P], F32, name="z_bank", tag="turn")
+                for j in range(NB - 1):
+                    nc.tensor.matmul(z_bank[:], lhsT=sums[j][:], rhs=ident[:], start=(j == 0), stop=False, is_transpose=True)
+        nc.tensor.matmul(z_bank[:], lhsT=sums[NB - 1][:], rhs=ident[:], start=False, stop=True, is_transpose=True)
+        z_rows = keep.tile([P, P], F32, name="z_rows")
+        nc.vector.tensor_scalar(out=z_rows[0:MB, :], in0=z_bank[0:MB, :], scalar1=1.0 / N, scalar2=None, op0=ALU.mult)
+        nc.scalar.dma_start(out=out_1.rearrange("(m p) o -> m (p o)", p=P), in_=z_rows[0:MB, :])

@@ -19,30 +19,34 @@ ALU = mybir.AluOpType
 P = 128
 PACK = 4
 K_PASS = P * PACK
+PAIRS = K_PASS // 2
 G = D // K_PASS
 NT = 512
 MB = M // P
 NB = N // NT
 RB = NT // P
 STEPS = MB * NB
-SCALAR_JOBS = 15
-PW = NT // 2
-WARM_UPS = 5
-SCALAR_U = 0
-PROMPT = 2
-RUN_STEPS = [0, 1, 3, 4, 5, 9, 13, 17, 21]
-U_STEP = -2
-P_STEPS = [4, 6, 10, 14, 18, 22]
+HALF = NT // 2
+RUN = 2
+GAP = MB // RB
+
+SCALAR_BLOCKS = 18
+K1_STEP = 4
+P1_STEP = 3
+U_LEAD = 2
+AHEAD = 1
+WARM_UPS = 4
+HOLD_UPS = 2
 
 
 def tile_softcapped_attention_weights_s2_kernel(tc, q, k, u, p, b, out_0, out_1):
     nc = tc.nc
     with ExitStack() as ctx:
         keep = ctx.enter_context(tc.tile_pool(name="keep", bufs=1))
-        stage = ctx.enter_context(tc.tile_pool(name="stage", bufs=5))
-        work = ctx.enter_context(tc.tile_pool(name="work", bufs=16))
+        stage = ctx.enter_context(tc.tile_pool(name="stage", bufs=6))
+        work = ctx.enter_context(tc.tile_pool(name="work", bufs=2 * MB))
         psum = ctx.enter_context(tc.psum_pool(name="psum", bufs=4))
-        ctx.enter_context(tc.manual_schedule(engines={mybir.EngineType.PE, mybir.EngineType.SP}))
+        ctx.enter_context(tc.manual_schedule())
 
         def mx_tiles(name, width):
             codes = keep.tile([P, width], U32, name=name + "_codes", align_bytes=64)
@@ -54,143 +58,155 @@ def tile_softcapped_attention_weights_s2_kernel(tc, q, k, u, p, b, out_0, out_1)
         u_mx = [mx_tiles("u%d" % m, P) for m in range(MB)]
         p_mx = [mx_tiles("p%d" % n, NT) for n in range(NB)]
 
-        ident = keep.tile([P, P], F32, name="ident")
-        make_identity(nc, ident[:])
-        ones = keep.tile([P, P], BF16, name="ones")
-        nc.vector.memset(ones[:], 1.0)
-        b_row = keep.tile([P, N], BF16, name="b_row")
         zeros = keep.tile([P, NT], BF16, name="zeros")
         nc.vector.memset(zeros[:], 0.0)
+        b_row = keep.tile([P, N], BF16, name="b_row")
         nc.vector.memset(b_row[:], 0.0)
+        ones = keep.tile([P, P], BF16, name="ones")
+        nc.vector.memset(ones[:], 1.0)
+        ident = keep.tile([P, P], F32, name="ident")
+        make_identity(nc, ident[:])
         idle = psum.tile([P, NT], F32, name="idle", tag="acc")
-        for i in range(WARM_UPS):
-            nc.tensor.matmul(idle[:], lhsT=ones[:], rhs=zeros[:], start=True, stop=True)
-        warm = keep.tile([P, 1], F32, name="warm")
-        nc.scalar.activation(out=warm[:], in_=ones[:, 0:1], func=ACT.Tanh)
+
+        def idle_matmuls(count):
+            for unused in range(count):
+                nc.tensor.matmul(idle[:], lhsT=zeros[:, 0:P], rhs=zeros[:], start=True, stop=True)
+
+        idle_matmuls(WARM_UPS)
+        table = keep.tile([P, 1], F32, name="table")
+        nc.scalar.activation(out=table[:], in_=zeros[:, 0:1], func=ACT.Tanh)
         sums = []
         for n in range(NB):
             sums_n = keep.tile([P, P], F32, name="sums%d" % n)
-            nc.gpsimd.memset(sums_n[:], 0.0)
+            nc.vector.memset(sums_n[:], 0.0)
             sums.append(sums_n)
 
-        jobs = [("k", 0, r) for r in range(RB)] + [("q", m, 0) for m in range(MB)]
-        jobs = jobs + [("k", n, r) for n in range(1, NB) for r in range(RB)]
+        k_blocks = [[("k", n, r) for r in range(RB)] for n in range(NB)]
+        q_blocks = [("q", m, 0) for m in range(MB)]
+        blocks = k_blocks[0] + q_blocks + [blk for n in range(1, NB) for blk in k_blocks[n]]
         raw, p_raw, u_raw = {}, {}, {}
 
-        def load_rows(job):
-            kind, i, r = job
-            rows = keep.tile([P, D], BF16, name="raw_%s%d_%d" % job)
+        def load_rows(blk):
+            kind, i, r = blk
+            rows = keep.tile([P, D], BF16, name="raw_%s%d_%d" % blk)
             src = q[i * P:(i + 1) * P, :] if kind == "q" else k[i * NT + r * P:i * NT + (r + 1) * P, :]
             nc.sync.dma_start(out=rows[:], in_=src)
-            raw[job] = rows
+            raw[blk] = rows
 
-        def load_p(n, h0, h1):
-            rows = keep.tile([P, PACK, (h1 - h0) * PW], BF16, name="p_raw%d_%d" % (n, h0))
-            src = p[:, n * NT + h0 * PW:n * NT + h1 * PW]
+        def load_columns(name, src):
+            rows = keep.tile([P, PACK, src.shape[1]], BF16, name=name)
             nc.sync.dma_start(out=rows[:], in_=src.rearrange("(p t) c -> p t c", t=PACK))
-            for h in range(h0, h1):
-                p_raw[(n, h)] = rows[:, :, (h - h0) * PW:(h - h0 + 1) * PW]
+            return rows
+
+        def load_p_half(h):
+            p_raw[(0, h)] = load_columns("p_raw0_%d" % h, p[:, h * HALF:(h + 1) * HALF])[:]
+
+        def load_p(n):
+            rows = load_columns("p_raw%d" % n, p[:, n * NT:(n + 1) * NT])
+            for r in range(RB):
+                p_raw[(n, r)] = rows[:, :, r * P:(r + 1) * P]
 
         def load_u(m0, m1):
-            rows = keep.tile([P, PACK, (m1 - m0) * P], BF16, name="u_raw%d" % m0)
-            nc.sync.dma_start(out=rows[:], in_=u[:, m0 * P:m1 * P].rearrange("(p t) c -> p t c", t=PACK))
+            rows = load_columns("u_raw%d" % m0, u[:, m0 * P:m1 * P])
             for m in range(m0, m1):
                 u_raw[m] = rows[:, :, (m - m0) * P:(m - m0 + 1) * P]
 
-        load_rows(jobs[0])
+        load_rows(k_blocks[0][0])
+        load_p_half(0)
         nc.sync.dma_start(out=b_row[0:1, :], in_=b.rearrange("(o n) -> o n", o=1))
-        load_p(0, 0, 1)
-        for job in jobs[1:RB + 1]:
-            load_rows(job)
-        load_p(0, 1, 2)
+        load_rows(k_blocks[0][1])
+        load_p_half(1)
+        for blk in k_blocks[0][2:] + q_blocks[:1]:
+            load_rows(blk)
         load_u(0, 1)
-        for job in jobs[RB + 1:RB + 3]:
-            load_rows(job)
+        load_rows(q_blocks[1])
         load_u(1, MB // 2)
-        for job in jobs[RB + 3:RB + MB // 2 + 2]:
-            load_rows(job)
+        for blk in q_blocks[2:MB - RUN]:
+            load_rows(blk)
         load_u(MB // 2, MB)
-        for job in jobs[RB + MB // 2 + 2:RB + MB]:
-            load_rows(job)
+        for blk in q_blocks[MB - RUN:]:
+            load_rows(blk)
         for n in range(1, NB):
-            load_p(n, 0, 2)
-            for r in range(RB):
-                load_rows(("k", n, r))
+            load_p(n)
+            for blk in k_blocks[n]:
+                load_rows(blk)
 
-        banks, turned, woven, acc, tiles = {}, {}, {}, {}, {}
-        bias = {}
+        turn_banks, turned, woven, bias_banks, bias, acc, tiles = {}, {}, {}, {}, {}, {}, {}
 
-        def transpose(job):
-            words = raw[job][:].bitcast(F32)
-            bank = psum.tile([P, G, 2, P], F32, name="bank", tag="turn")
+        def turn(blk):
+            words = raw[blk][:].bitcast(F32)
+            bank = psum.tile([P, G, 2, P], F32, name="turn_bank", tag="turn")
             for g in range(G):
                 for h in range(2):
-                    nc.tensor.transpose(bank[:, g, h, :], words[:, 256 * g + h:256 * (g + 1):2], ident[:])
-            banks[job] = bank
+                    nc.tensor.transpose(bank[:, g, h, :], words[:, PAIRS * g + h:PAIRS * (g + 1):2], ident[:])
+            turn_banks[blk] = bank
 
-        def copy_out(job):
+        def copy_out(blk):
             dst = stage.tile([P, G * P * PACK], BF16, name="turned", align_bytes=64)
             view = dst[:].bitcast(F32).rearrange("p (g r h) -> p g r h", g=G, h=2)
-            src = banks[job][:].rearrange("p g h r -> p g r h")
-            if jobs.index(job) < SCALAR_JOBS:
+            src = turn_banks[blk][:].rearrange("p g h r -> p g r h")
+            if blocks.index(blk) < SCALAR_BLOCKS:
                 nc.scalar.copy(out=view, in_=src)
             else:
                 nc.vector.tensor_copy(out=view, in_=src)
-            turned[job] = dst
+            turned[blk] = dst
 
-        def quantize_rows(job):
-            kind, i, r = job
+        def quantize_rows(blk):
+            kind, i, r = blk
             if kind == "q":
                 codes, scales = q_mx[i]
-                nc.vector.quantize_mx(out=codes[:].bitcast(E4M3X4), scales=scales[:], in_=turned[job][:])
+                nc.vector.quantize_mx(out=codes[:].bitcast(E4M3X4), scales=scales[:], in_=turned[blk][:])
             else:
+                cols = slice(r * P, (r + 1) * P)
                 for g in range(G):
                     codes, scales = k_mx[i][g]
-                    cols = slice(r * P, (r + 1) * P)
                     nc.vector.quantize_mx(out=codes[:, cols].bitcast(E4M3X4), scales=scales[:, cols],
-                                          in_=turned[job][:, g * K_PASS:(g + 1) * K_PASS])
+                                          in_=turned[blk][:, g * K_PASS:(g + 1) * K_PASS])
 
-        def weave(key, src, copy):
+        def weave(key, src):
             width = src.shape[2]
             dst = stage.tile([P, width * PACK], BF16, name="woven_%s%d" % (key[0], width), align_bytes=64)
-            copy(out=dst[:].rearrange("p (c i t) -> p c t i", i=4, t=PACK), in_=src.rearrange("p t (c i) -> p c t i", i=4))
+            nc.vector.tensor_copy(out=dst[:].rearrange("p (c i t) -> p c t i", i=4, t=PACK),
+                                  in_=src.rearrange("p t (c i) -> p c t i", i=4))
             woven[key] = dst
 
         def weave_u(m):
-            weave(("u", m), u_raw[m], nc.scalar.copy if m < SCALAR_U else nc.vector.tensor_copy)
+            weave(("u", m), u_raw[m])
 
-        def weave_p(n, h):
-            weave(("p", n, h), p_raw[(n, h)], nc.vector.tensor_copy)
+        def weave_p(n, piece):
+            weave(("p", n, piece), p_raw[(n, piece)])
 
         def quantize_u(m):
             codes, scales = u_mx[m]
             nc.vector.quantize_mx(out=codes[:].bitcast(E5M2X4), scales=scales[:], in_=woven[("u", m)][:])
 
-        def quantize_p(n, h):
+        def quantize_p(n, piece):
             codes, scales = p_mx[n]
-            cols = slice(h * PW, (h + 1) * PW)
-            nc.vector.quantize_mx(out=codes[:, cols].bitcast(E4M3X4), scales=scales[:, cols], in_=woven[("p", n, h)][:])
+            width = p_raw[(n, piece)].shape[2]
+            cols = slice(piece * width, (piece + 1) * width)
+            nc.vector.quantize_mx(out=codes[:, cols].bitcast(E4M3X4), scales=scales[:, cols],
+                                  in_=woven[("p", n, piece)][:])
 
         def spread_bias(n):
             bank = psum.tile([P, NT], BF16, name="bias_bank", tag="acc")
             nc.tensor.matmul(bank[:], lhsT=ones[:], rhs=b_row[:, n * NT:(n + 1) * NT], start=True, stop=True)
-            banks[n] = bank
+            bias_banks[n] = bank
 
         def keep_bias(n):
             bias_n = keep.tile([P, NT], BF16, name="bias%d" % n)
-            nc.scalar.copy(out=bias_n[:], in_=banks[n][:])
+            nc.scalar.copy(out=bias_n[:], in_=bias_banks[n][:])
             bias[n] = bias_n
 
         def multiply(s):
             n, m = divmod(s, MB)
             bank = psum.tile([P, NT], F32, name="acc", tag="acc")
+            nc.tensor.matmul_mx(out=bank[:], lhsT=u_mx[m][0][:].bitcast(E5M2X4), lhsT_scale=u_mx[m][1][:],
+                                rhs=p_mx[n][0][:].bitcast(E4M3X4), rhs_scale=p_mx[n][1][:], start=True, stop=False)
             for g in range(G):
                 cols = slice(g * P, (g + 1) * P)
-                nc.tensor.matmul_mx(out=bank[:], lhsT=q_mx[m][0][:, cols].bitcast(E4M3X4), lhsT_scale=q_mx[m][1][:, cols],
-                                    rhs=k_mx[n][g][0][:].bitcast(E4M3X4), rhs_scale=k_mx[n][g][1][:],
-                                    start=(g == 0), stop=False)
-            nc.tensor.matmul_mx(out=bank[:], lhsT=u_mx[m][0][:].bitcast(E5M2X4), lhsT_scale=u_mx[m][1][:],
-                                rhs=p_mx[n][0][:].bitcast(E4M3X4), rhs_scale=p_mx[n][1][:], start=False, stop=True)
+                nc.tensor.matmul_mx(out=bank[:], lhsT=q_mx[m][0][:, cols].bitcast(E4M3X4),
+                                    lhsT_scale=q_mx[m][1][:, cols], rhs=k_mx[n][g][0][:].bitcast(E4M3X4),
+                                    rhs_scale=k_mx[n][g][1][:], start=False, stop=(g == G - 1))
             acc[s] = bank
 
         def add_bias(s):
@@ -198,7 +214,7 @@ def tile_softcapped_attention_weights_s2_kernel(tc, q, k, u, p, b, out_0, out_1)
             nc.vector.tensor_tensor(out=logits[:], in0=acc[s][:], in1=bias[s // MB][:], op=ALU.add)
             tiles[s] = logits
 
-        def cap(s):
+        def limit(s):
             nc.scalar.activation(out=tiles[s][:], in_=tiles[s][:], func=ACT.Tanh, scale=1.0 / CAP)
 
         def weigh(s):
@@ -207,80 +223,85 @@ def tile_softcapped_attention_weights_s2_kernel(tc, q, k, u, p, b, out_0, out_1)
                                  accum_out=sums[n][:, m:m + 1])
             nc.sync.dma_start(out=out_0[m * P:(m + 1) * P, n * NT:(n + 1) * NT], in_=tiles[s][:])
 
-        k0 = jobs[:RB]
-        q0, q1, q2 = jobs[RB:RB + 3]
-        transpose(k0[0])
-        for n in range(NB):
-            spread_bias(n)
+        k0 = k_blocks[0]
+        turn(k0[0])
         copy_out(k0[0])
-        for n in range(NB):
-            keep_bias(n)
         weave_p(0, 0)
+        for n in range(NB // 2):
+            spread_bias(n)
+            keep_bias(n)
         quantize_rows(k0[0])
         quantize_p(0, 0)
-        for job in k0[1:3]:
-            transpose(job)
-            copy_out(job)
-            quantize_rows(job)
-        for job in (k0[3], q0):
-            transpose(job)
-            copy_out(job)
+        turn(k0[1])
+        idle_matmuls(HOLD_UPS)
+        copy_out(k0[1])
         weave_p(0, 1)
+        quantize_rows(k0[1])
+        quantize_p(0, 1)
+        for blk in (k0[2], k0[3], q_blocks[0]):
+            turn(blk)
+            copy_out(blk)
+        for n in range(NB // 2, NB):
+            spread_bias(n)
+        turn(q_blocks[1])
+        copy_out(q_blocks[1])
+        for n in range(NB // 2, NB):
+            keep_bias(n)
+        quantize_rows(k0[2])
         weave_u(0)
         quantize_rows(k0[3])
-        quantize_rows(q0)
-        quantize_p(0, 1)
         quantize_u(0)
-        for job in (q1, q2):
-            transpose(job)
-            copy_out(job)
+        quantize_rows(q_blocks[0])
         weave_u(1)
-        quantize_rows(q1)
+        quantize_rows(q_blocks[1])
         quantize_u(1)
-        quantize_rows(q2)
 
-        rest = jobs[RB + 3:]
-        turn_at = {job: RUN_STEPS[j // 2] for j, job in enumerate(rest)}
-        copy_at = {job: turn_at[job] + (0 if turn_at[job] < PROMPT else 1) for job in rest}
-        u_at = {m: m + U_STEP for m in range(2, MB)}
-        p_at = {(n, h): P_STEPS[2 * (n - 1) + h] for n in range(1, NB) for h in range(2)}
-        z_bank = None
-        for t in range(STEPS + 3):
-            s = t
-            if 0 <= s < STEPS:
+        turn_at, copy_at, p_at = {}, {}, {}
+        for j, blk in enumerate(q_blocks[2:]):
+            turn_at[blk] = j // RUN
+            copy_at[blk] = j // RUN + (0 if j < RUN else 1)
+        u_at = {m: m - U_LEAD for m in range(2, MB)}
+        for r, blk in enumerate(k_blocks[1]):
+            turn_at[blk] = K1_STEP + r // RUN
+            copy_at[blk] = turn_at[blk] + 1
+            p_at[(1, r)] = P1_STEP + r
+        for n in range(2, NB):
+            for r, blk in enumerate(k_blocks[n]):
+                copy_at[blk] = (n - 1) * MB - AHEAD + r * GAP
+                turn_at[blk] = (n - 1) * MB - AHEAD + r // RUN * RUN * GAP - 1
+                p_at[(n, r)] = copy_at[blk]
+
+        def due(steps, s):
+            return [key for key in steps if steps[key] == s]
+
+        for s in range(STEPS + 3):
+            if s < STEPS:
                 multiply(s)
-            for job in rest:
-                if turn_at[job] == t:
-                    transpose(job)
-            if 0 <= s - 1 < STEPS:
+            for blk in due(turn_at, s):
+                turn(blk)
+            if 1 <= s < STEPS + 1:
                 add_bias(s - 1)
-            if 0 <= s - 2 < STEPS:
-                cap(s - 2)
-            if 0 <= s - 3 < STEPS:
+            if 2 <= s < STEPS + 2:
+                limit(s - 2)
+            if 3 <= s:
                 weigh(s - 3)
-            for piece in p_at:
-                if p_at[piece] == t - 1:
-                    quantize_p(*piece)
-            for m in u_at:
-                if u_at[m] == t - 1:
-                    quantize_u(m)
-            for job in rest:
-                if copy_at[job] == t - 1:
-                    quantize_rows(job)
-            for job in rest:
-                if copy_at[job] == t:
-                    copy_out(job)
-            for piece in p_at:
-                if p_at[piece] == t:
-                    weave_p(*piece)
-            for m in u_at:
-                if u_at[m] == t:
-                    weave_u(m)
-            if s == STEPS:
-                z_bank = psum.tile([P, P], F32, name="z_bank", tag="turn")
-                for j in range(NB - 1):
-                    nc.tensor.matmul(z_bank[:], lhsT=sums[j][:], rhs=ident[:], start=(j == 0), stop=False, is_transpose=True)
-        nc.tensor.matmul(z_bank[:], lhsT=sums[NB - 1][:], rhs=ident[:], start=False, stop=True, is_transpose=True)
+            for piece in due(p_at, s - 1):
+                quantize_p(*piece)
+            for m in due(u_at, s - 1):
+                quantize_u(m)
+            for blk in due(copy_at, s - 1):
+                quantize_rows(blk)
+            for blk in due(copy_at, s):
+                copy_out(blk)
+            for piece in due(p_at, s):
+                weave_p(*piece)
+            for m in due(u_at, s):
+                weave_u(m)
+
+        z_bank = psum.tile([P, P], F32, name="z_bank", tag="turn")
+        for n in range(NB):
+            nc.tensor.matmul(z_bank[:], lhsT=sums[n][:], rhs=ident[:], start=(n == 0), stop=(n == NB - 1),
+                             is_transpose=True)
         z_rows = keep.tile([P, P], F32, name="z_rows")
         nc.vector.tensor_scalar(out=z_rows[0:MB, :], in0=z_bank[0:MB, :], scalar1=1.0 / N, scalar2=None, op0=ALU.mult)
         nc.scalar.dma_start(out=out_1.rearrange("(m p) o -> m (p o)", p=P), in_=z_rows[0:MB, :])

@@ -35,8 +35,6 @@ K1_STEP = 4
 P1_STEP = 3
 U_LEAD = 2
 AHEAD = 1
-WARM_UPS = 4
-HOLD_UPS = 2
 
 
 def tile_softcapped_attention_weights_s2_kernel(tc, q, k, u, p, b, out_0, out_1):
@@ -58,7 +56,7 @@ def tile_softcapped_attention_weights_s2_kernel(tc, q, k, u, p, b, out_0, out_1)
         u_mx = [mx_tiles("u%d" % m, P) for m in range(MB)]
         p_mx = [mx_tiles("p%d" % n, NT) for n in range(NB)]
 
-        zeros = keep.tile([P, NT], BF16, name="zeros")
+        zeros = keep.tile([P, P], BF16, name="zeros")
         nc.vector.memset(zeros[:], 0.0)
         b_row = keep.tile([P, N], BF16, name="b_row")
         nc.vector.memset(b_row[:], 0.0)
@@ -66,19 +64,10 @@ def tile_softcapped_attention_weights_s2_kernel(tc, q, k, u, p, b, out_0, out_1)
         nc.vector.memset(ones[:], 1.0)
         ident = keep.tile([P, P], F32, name="ident")
         make_identity(nc, ident[:])
-        idle = psum.tile([P, NT], F32, name="idle", tag="acc")
-
-        def idle_matmuls(count):
-            for unused in range(count):
-                nc.tensor.matmul(idle[:], lhsT=zeros[:, 0:P], rhs=zeros[:], start=True, stop=True)
-
-        idle_matmuls(WARM_UPS)
-        table = keep.tile([P, 1], F32, name="table")
-        nc.scalar.activation(out=table[:], in_=zeros[:, 0:1], func=ACT.Tanh)
         sums = []
         for n in range(NB):
             sums_n = keep.tile([P, P], F32, name="sums%d" % n)
-            nc.vector.memset(sums_n[:], 0.0)
+            nc.scalar.activation(out=sums_n[:], in_=zeros[:], func=ACT.Tanh)
             sums.append(sums_n)
 
         k_blocks = [[("k", n, r) for r in range(RB)] for n in range(NB)]
@@ -233,7 +222,6 @@ def tile_softcapped_attention_weights_s2_kernel(tc, q, k, u, p, b, out_0, out_1)
         quantize_rows(k0[0])
         quantize_p(0, 0)
         turn(k0[1])
-        idle_matmuls(HOLD_UPS)
         copy_out(k0[1])
         weave_p(0, 1)
         quantize_rows(k0[1])

@@ -30,11 +30,10 @@ HALF = NT // 2
 RUN = 2
 GAP = MB // RB
 
-SCALAR_BLOCKS = 18
+SCALAR_BLOCKS = 16
 K1_STEP = 4
 P1_STEP = 3
 U_LEAD = 2
-AHEAD = 1
 
 
 def tile_softcapped_attention_weights_s2_kernel(tc, q, k, u, p, b, out_0, out_1):
@@ -165,6 +164,13 @@ def tile_softcapped_attention_weights_s2_kernel(tc, q, k, u, p, b, out_0, out_1)
         def weave_p(n, piece):
             weave(("p", n, piece), p_raw[(n, piece)])
 
+        def weave_p_on_gpsimd(n, piece):
+            dst = stage.tile([P, P * PACK], BF16, name="woven_late", align_bytes=64, bufs=1)
+            nc.gpsimd.tensor_scalar(out=dst[:].rearrange("p (c t) -> p c t", t=PACK),
+                                    in0=p_raw[(n, piece)].rearrange("p t c -> p c t"),
+                                    scalar1=1.0, scalar2=0.0, op0=ALU.mult, op1=ALU.add)
+            woven[("p", n, piece)] = dst
+
         def quantize_u(m):
             codes, scales = u_mx[m]
             nc.vector.quantize_mx(out=codes[:].bitcast(E5M2X4), scales=scales[:], in_=woven[("u", m)][:])
@@ -244,7 +250,7 @@ def tile_softcapped_attention_weights_s2_kernel(tc, q, k, u, p, b, out_0, out_1)
         quantize_rows(q_blocks[1])
         quantize_u(1)
 
-        turn_at, copy_at, p_at = {}, {}, {}
+        turn_at, copy_at, p_at, late_p_at = {}, {}, {}, {}
         for j, blk in enumerate(q_blocks[2:]):
             turn_at[blk] = j // RUN
             copy_at[blk] = j // RUN + (0 if j < RUN else 1)
@@ -255,9 +261,9 @@ def tile_softcapped_attention_weights_s2_kernel(tc, q, k, u, p, b, out_0, out_1)
             p_at[(1, r)] = P1_STEP + r
         for n in range(2, NB):
             for r, blk in enumerate(k_blocks[n]):
-                copy_at[blk] = (n - 1) * MB - AHEAD + r * GAP
-                turn_at[blk] = (n - 1) * MB - AHEAD + r // RUN * RUN * GAP - 1
-                p_at[(n, r)] = copy_at[blk]
+                copy_at[blk] = (n - 1) * MB + r * GAP
+                turn_at[blk] = (n - 1) * MB + r // RUN * RUN * GAP - 1
+                late_p_at[(n, r)] = copy_at[blk]
 
         def due(steps, s):
             return [key for key in steps if steps[key] == s]
@@ -279,10 +285,14 @@ def tile_softcapped_attention_weights_s2_kernel(tc, q, k, u, p, b, out_0, out_1)
                 quantize_u(m)
             for blk in due(copy_at, s - 1):
                 quantize_rows(blk)
+            for piece in due(late_p_at, s - 1):
+                quantize_p(*piece)
             for blk in due(copy_at, s):
                 copy_out(blk)
             for piece in due(p_at, s):
                 weave_p(*piece)
+            for piece in due(late_p_at, s):
+                weave_p_on_gpsimd(*piece)
             for m in due(u_at, s):
                 weave_u(m)
 

from contextlib import ExitStack

import concourse.mybir as mybir
from concourse.masks import make_identity

M, N, D, H = 1024, 2048, 1024, 512
FLOPS = 2 * M * N * (D + H)
CAP = 2.0

F32 = mybir.dt.float32
BF16 = mybir.dt.bfloat16
U32 = mybir.dt.uint32
U8 = mybir.dt.uint8
E4M3X4 = mybir.dt.float8_e4m3fn_x4
E5M2X4 = mybir.dt.float8_e5m2_x4
ACT = mybir.ActivationFunctionType
ALU = mybir.AluOpType

P = 128
PACK = 4
K_PASS = P * PACK
PAIRS = K_PASS // 2
G = D // K_PASS
NT = 512
MB = M // P
NB = N // NT
RB = NT // P
STEPS = MB * NB
HALF = NT // 2
RUN = 2
GAP = MB // RB

SCALAR_BLOCKS = 16
K1_STEP = 4
P1_STEP = 3
U_LEAD = 2


def tile_softcapped_attention_weights_s2_kernel(tc, q, k, u, p, b, out_0, out_1):
    nc = tc.nc
    with ExitStack() as ctx:
        keep = ctx.enter_context(tc.tile_pool(name="keep", bufs=1))
        stage = ctx.enter_context(tc.tile_pool(name="stage", bufs=6))
        work = ctx.enter_context(tc.tile_pool(name="work", bufs=2 * MB))
        psum = ctx.enter_context(tc.psum_pool(name="psum", bufs=4))
        ctx.enter_context(tc.manual_schedule())

        def mx_tiles(name, width):
            codes = keep.tile([P, width], U32, name=name + "_codes", align_bytes=64)
            scales = keep.tile([P, width], U8, name=name + "_scales", align_bytes=64)
            return codes, scales

        q_mx = [mx_tiles("q%d" % m, G * P) for m in range(MB)]
        k_mx = [[mx_tiles("k%d_%d" % (n, g), NT) for g in range(G)] for n in range(NB)]
        u_mx = [mx_tiles("u%d" % m, P) for m in range(MB)]
        p_mx = [mx_tiles("p%d" % n, NT) for n in range(NB)]

        zeros = keep.tile([P, P], BF16, name="zeros")
        nc.vector.memset(zeros[:], 0.0)
        b_row = keep.tile([P, N], BF16, name="b_row")
        nc.vector.memset(b_row[:], 0.0)
        ones = keep.tile([P, P], BF16, name="ones")
        nc.vector.memset(ones[:], 1.0)
        ident = keep.tile([P, P], F32, name="ident")
        make_identity(nc, ident[:])
        sums = []
        for n in range(NB):
            sums_n = keep.tile([P, P], F32, name="sums%d" % n)
            nc.scalar.activation(out=sums_n[:], in_=zeros[:], func=ACT.Tanh)
            sums.append(sums_n)

        k_blocks = [[("k", n, r) for r in range(RB)] for n in range(NB)]
        q_blocks = [("q", m, 0) for m in range(MB)]
        blocks = k_blocks[0] + q_blocks + [blk for n in range(1, NB) for blk in k_blocks[n]]
        raw, p_raw, u_raw = {}, {}, {}

        def load_rows(blk):
            kind, i, r = blk
            rows = keep.tile([P, D], BF16, name="raw_%s%d_%d" % blk)
            src = q[i * P:(i + 1) * P, :] if kind == "q" else k[i * NT + r * P:i * NT + (r + 1) * P, :]
            nc.sync.dma_start(out=rows[:], in_=src)
            raw[blk] = rows

        def load_columns(name, src):
            rows = keep.tile([P, PACK, src.shape[1]], BF16, name=name)
            nc.sync.dma_start(out=rows[:], in_=src.rearrange("(p t) c -> p t c", t=PACK))
            return rows

        def load_p_half(h):
            p_raw[(0, h)] = load_columns("p_raw0_%d" % h, p[:, h * HALF:(h + 1) * HALF])[:]

        def load_p(n):
            rows = load_columns("p_raw%d" % n, p[:, n * NT:(n + 1) * NT])
            for r in range(RB):
                p_raw[(n, r)] = rows[:, :, r * P:(r + 1) * P]

        def load_u(m0, m1):
            rows = load_columns("u_raw%d" % m0, u[:, m0 * P:m1 * P])
            for m in range(m0, m1):
                u_raw[m] = rows[:, :, (m - m0) * P:(m - m0 + 1) * P]

        load_rows(k_blocks[0][0])
        load_p_half(0)
        nc.sync.dma_start(out=b_row[0:1, :], in_=b.rearrange("(o n) -> o n", o=1))
        load_rows(k_blocks[0][1])
        load_p_half(1)
        for blk in k_blocks[0][2:] + q_blocks[:1]:
            load_rows(blk)
        load_u(0, 1)
        load_rows(q_blocks[1])
        load_u(1, MB // 2)
        for blk in q_blocks[2:MB - RUN]:
            load_rows(blk)
        load_u(MB // 2, MB)
        for blk in q_blocks[MB - RUN:]:
            load_rows(blk)
        for n in range(1, NB):
            load_p(n)
            for blk in k_blocks[n]:
                load_rows(blk)

        turn_banks, turned, woven, bias_banks, bias, acc, tiles = {}, {}, {}, {}, {}, {}, {}

        def turn(blk):
            words = raw[blk][:].bitcast(F32)
            bank = psum.tile([P, G, 2, P], F32, name="turn_bank", tag="turn")
            for g in range(G):
                for h in range(2):
                    nc.tensor.transpose(bank[:, g, h, :], words[:, PAIRS * g + h:PAIRS * (g + 1):2], ident[:])
            turn_banks[blk] = bank

        def copy_out(blk):
            dst = stage.tile([P, G * P * PACK], BF16, name="turned", align_bytes=64)
            view = dst[:].bitcast(F32).rearrange("p (g r h) -> p g r h", g=G, h=2)
            src = turn_banks[blk][:].rearrange("p g h r -> p g r h")
            if blocks.index(blk) < SCALAR_BLOCKS:
                nc.scalar.copy(out=view, in_=src)
            else:
                nc.vector.tensor_copy(out=view, in_=src)
            turned[blk] = dst

        def quantize_rows(blk):
            kind, i, r = blk
            if kind == "q":
                codes, scales = q_mx[i]
                nc.vector.quantize_mx(out=codes[:].bitcast(E4M3X4), scales=scales[:], in_=turned[blk][:])
            else:
                cols = slice(r * P, (r + 1) * P)
                for g in range(G):
                    codes, scales = k_mx[i][g]
                    nc.vector.quantize_mx(out=codes[:, cols].bitcast(E4M3X4), scales=scales[:, cols],
                                          in_=turned[blk][:, g * K_PASS:(g + 1) * K_PASS])

        def weave(key, src):
            width = src.shape[2]
            dst = stage.tile([P, width * PACK], BF16, name="woven_%s%d" % (key[0], width), align_bytes=64)
            nc.vector.tensor_copy(out=dst[:].rearrange("p (c i t) -> p c t i", i=4, t=PACK),
                                  in_=src.rearrange("p t (c i) -> p c t i", i=4))
            woven[key] = dst

        def weave_u(m):
            weave(("u", m), u_raw[m])

        def weave_p(n, piece):
            weave(("p", n, piece), p_raw[(n, piece)])

        def weave_p_on_gpsimd(n, piece):
            dst = stage.tile([P, P * PACK], BF16, name="woven_late", align_bytes=64, bufs=1)
            nc.gpsimd.tensor_scalar(out=dst[:].rearrange("p (c t) -> p c t", t=PACK),
                                    in0=p_raw[(n, piece)].rearrange("p t c -> p c t"),
                                    scalar1=1.0, scalar2=0.0, op0=ALU.mult, op1=ALU.add)
            woven[("p", n, piece)] = dst

        def quantize_u(m):
            codes, scales = u_mx[m]
            nc.vector.quantize_mx(out=codes[:].bitcast(E5M2X4), scales=scales[:], in_=woven[("u", m)][:])

        def quantize_p(n, piece):
            codes, scales = p_mx[n]
            width = p_raw[(n, piece)].shape[2]
            cols = slice(piece * width, (piece + 1) * width)
            nc.vector.quantize_mx(out=codes[:, cols].bitcast(E4M3X4), scales=scales[:, cols],
                                  in_=woven[("p", n, piece)][:])

        def spread_bias(n):
            bank = psum.tile([P, NT], BF16, name="bias_bank", tag="acc")
            nc.tensor.matmul(bank[:], lhsT=ones[:], rhs=b_row[:, n * NT:(n + 1) * NT], start=True, stop=True)
            bias_banks[n] = bank

        def keep_bias(n):
            bias_n = keep.tile([P, NT], BF16, name="bias%d" % n)
            nc.scalar.copy(out=bias_n[:], in_=bias_banks[n][:])
            bias[n] = bias_n

        def multiply(s):
            n, m = divmod(s, MB)
            bank = psum.tile([P, NT], F32, name="acc", tag="acc")
            nc.tensor.matmul_mx(out=bank[:], lhsT=u_mx[m][0][:].bitcast(E5M2X4), lhsT_scale=u_mx[m][1][:],
                                rhs=p_mx[n][0][:].bitcast(E4M3X4), rhs_scale=p_mx[n][1][:], start=True, stop=False)
            for g in range(G):
                cols = slice(g * P, (g + 1) * P)
                nc.tensor.matmul_mx(out=bank[:], lhsT=q_mx[m][0][:, cols].bitcast(E4M3X4),
                                    lhsT_scale=q_mx[m][1][:, cols], rhs=k_mx[n][g][0][:].bitcast(E4M3X4),
                                    rhs_scale=k_mx[n][g][1][:], start=False, stop=(g == G - 1))
            acc[s] = bank

        def add_bias(s):
            logits = work.tile([P, NT], F32, name="logits")
            nc.vector.tensor_tensor(out=logits[:], in0=acc[s][:], in1=bias[s // MB][:], op=ALU.add)
            tiles[s] = logits

        def limit(s):
            nc.scalar.activation(out=tiles[s][:], in_=tiles[s][:], func=ACT.Tanh, scale=1.0 / CAP)

        def weigh(s):
            n, m = divmod(s, MB)
            nc.scalar.activation(out=tiles[s][:], in_=tiles[s][:], func=ACT.Exp, scale=CAP,
                                 accum_out=sums[n][:, m:m + 1])
            nc.sync.dma_start(out=out_0[m * P:(m + 1) * P, n * NT:(n + 1) * NT], in_=tiles[s][:])

        k0 = k_blocks[0]
        turn(k0[0])
        copy_out(k0[0])
        weave_p(0, 0)
        for n in range(NB // 2):
            spread_bias(n)
            keep_bias(n)
        quantize_rows(k0[0])
        quantize_p(0, 0)
        turn(k0[1])
        copy_out(k0[1])
        weave_p(0, 1)
        quantize_rows(k0[1])
        quantize_p(0, 1)
        for blk in (k0[2], k0[3], q_blocks[0]):
            turn(blk)
            copy_out(blk)
        for n in range(NB // 2, NB):
            spread_bias(n)
        turn(q_blocks[1])
        copy_out(q_blocks[1])
        for n in range(NB // 2, NB):
            keep_bias(n)
        quantize_rows(k0[2])
        weave_u(0)
        quantize_rows(k0[3])
        quantize_u(0)
        quantize_rows(q_blocks[0])
        weave_u(1)
        quantize_rows(q_blocks[1])
        quantize_u(1)

        turn_at, copy_at, p_at, late_p_at = {}, {}, {}, {}
        for j, blk in enumerate(q_blocks[2:]):
            turn_at[blk] = j // RUN
            copy_at[blk] = j // RUN + (0 if j < RUN else 1)
        u_at = {m: m - U_LEAD for m in range(2, MB)}
        for r, blk in enumerate(k_blocks[1]):
            turn_at[blk] = K1_STEP + r // RUN
            copy_at[blk] = turn_at[blk] + 1
            p_at[(1, r)] = P1_STEP + r
        for n in range(2, NB):
            for r, blk in enumerate(k_blocks[n]):
                copy_at[blk] = (n - 1) * MB + r * GAP
                turn_at[blk] = (n - 1) * MB + r // RUN * RUN * GAP - 1
                late_p_at[(n, r)] = copy_at[blk]

        def due(steps, s):
            return [key for key in steps if steps[key] == s]

        for s in range(STEPS + 3):
            if s < STEPS:
                multiply(s)
            for blk in due(turn_at, s):
                turn(blk)
            if 1 <= s < STEPS + 1:
                add_bias(s - 1)
            if 2 <= s < STEPS + 2:
                limit(s - 2)
            if 3 <= s:
                weigh(s - 3)
            for piece in due(p_at, s - 1):
                quantize_p(*piece)
            for m in due(u_at, s - 1):
                quantize_u(m)
            for blk in due(copy_at, s - 1):
                quantize_rows(blk)
            for piece in due(late_p_at, s - 1):
                quantize_p(*piece)
            for blk in due(copy_at, s):
                copy_out(blk)
            for piece in due(p_at, s):
                weave_p(*piece)
            for piece in due(late_p_at, s):
                weave_p_on_gpsimd(*piece)
            for m in due(u_at, s):
                weave_u(m)

        z_bank = psum.tile([P, P], F32, name="z_bank", tag="turn")
        for n in range(NB):
            nc.tensor.matmul(z_bank[:], lhsT=sums[n][:], rhs=ident[:], start=(n == 0), stop=(n == NB - 1),
                             is_transpose=True)
        z_rows = keep.tile([P, P], F32, name="z_rows")
        nc.vector.tensor_scalar(out=z_rows[0:MB, :], in0=z_bank[0:MB, :], scalar1=1.0 / N, scalar2=None, op0=ALU.mult)
        nc.scalar.dma_start(out=out_1.rearrange("(m p) o -> m (p o)", p=P), in_=z_rows[0:MB, :])
